import numpy as np
import ml_dtypes


def mxq(x, axis, fmt="e4m3"):
    dtype, down = {"e4m3": (ml_dtypes.float8_e4m3fn, 7), "e5m2": (ml_dtypes.float8_e5m2, 14)}[fmt]
    v = np.moveaxis(np.asarray(x, np.float32).astype(ml_dtypes.bfloat16).astype(np.float64), axis, -1)
    blocks = v.reshape(v.shape[:-1] + (-1, 32))
    amax = np.abs(blocks).max(-1, keepdims=True)
    byte = np.maximum(np.where(amax > 0, np.frexp(amax)[1] - 1 + 127, 0) - down, 1)
    scale = np.exp2(byte - 127.0)
    codes = (blocks / scale).astype(np.float32).astype(dtype).astype(np.float64)
    return np.moveaxis((codes * scale).reshape(v.shape), -1, axis)


WIDE = False


def mx_kscale(k):
    if not WIDE:
        return np.ones(k)
    levels = np.array([24, -24, 12, -12, 0])
    if k % 512:
        return np.exp2(np.random.permutation(np.resize(levels, k // 32))).repeat(32)
    a = np.empty((k // 512, 16))
    for p in range(k // 512):
        a[p, :8] = np.random.permutation(np.resize(levels, 8))
        for g in range(8):
            far = levels[np.abs(levels - a[p, g]) >= 10]
            a[p, g + 8] = far[np.random.randint(len(far))]
    return np.exp2(a.ravel()).repeat(32)


def f64(x):
    return np.asarray(x).astype(np.float64)


def striped(idx):
    return np.tile(idx.reshape(-1, 16).T, (8, 1)).astype(np.uint16)


def unstriped(offs):
    return offs[:16].T.reshape(-1).astype(np.int64)


E2M1 = np.array([0.0, 0.5, 1.0, 1.5, 2.0, 3.0, 4.0, 6.0, -0.0, -0.5, -1.0, -1.5, -2.0, -3.0, -4.0, -6.0])


def pack_weight(w, fmt):
    k, n = w.shape
    w = f64(np.asarray(w, np.float32).astype(ml_dtypes.bfloat16)).reshape(k // 32, 32, n)
    amax = np.abs(w).max(1)
    if fmt == "e4m3":
        byte = np.frexp(amax)[1] - 1 + 127 - 7
    else:
        mant, ex = np.frexp(amax / 6.0)
        byte = np.where(mant > 0.5, ex, ex - 1) + 127
    byte = np.clip(np.where(amax > 0, byte, 1), 1, 254)
    scaled = (w * np.exp2(127.0 - byte)[:, None, :]).reshape(k, n).astype(np.float32)
    by_word = np.ascontiguousarray(scaled.reshape(k // 512, 128, 4, n).transpose(0, 1, 3, 2))
    if fmt == "e4m3":
        words = by_word.astype(ml_dtypes.float8_e4m3fn).view(np.uint8)
    else:
        c = by_word.astype(ml_dtypes.float4_e2m1fn).view(np.uint8) & 0xF
        words = (c[..., 0::2] | (c[..., 1::2] << 4)).reshape(k // 512, 128, 2 * n)
    return np.ascontiguousarray(words), np.ascontiguousarray(byte.astype(np.uint8).reshape(k // 512, 16, n))


def unpack_weight(words, scales, fmt):
    g, _, n = scales.shape
    words = np.ascontiguousarray(words).reshape(g, 128, n, -1)
    if fmt == "e4m3":
        vals = words.view(ml_dtypes.float8_e4m3fn).astype(np.float64)
    else:
        nib = np.empty((g, 128, n, 4), np.uint8)
        nib[..., 0::2] = words & 0xF
        nib[..., 1::2] = words >> 4
        vals = E2M1[nib]
    vals = vals * np.repeat(np.exp2(scales.astype(np.float64) - 127.0), 8, axis=1)[..., None]
    return vals.transpose(0, 1, 3, 2).reshape(g * 512, n)


def silu(f):
    return f / (1.0 + np.exp(-np.maximum(f, -700.0)))


K, R, T, M, J = 1024, 1024, 2048, 512, 1024


def setup_inputs():
    n = np.random.standard_normal
    s = mx_kscale(K)[:, None]
    u = mx_kscale(R)[:, None]
    p_tab = pack_weight(n((K, T)) * s, "e4m3")
    p_tab2 = pack_weight(n((K, T)) * s, "e4m3")
    p_wa = pack_weight(n((K, R)) / np.sqrt(K) / s, "e2m1")
    return {
        "tab_words": p_tab[0],
        "tab_scales": p_tab[1],
        "tab2_words": p_tab2[0],
        "tab2_scales": p_tab2[1],
        "wa_words": p_wa[0],
        "wa_scales": p_wa[1],
        "wb": (n((K, R)) / np.sqrt(K) / s).astype(np.float32),
        "sa": (np.random.uniform(0.5, 2.0, R) * u[:, 0]).astype(np.float32),
        "sb": (np.random.uniform(0.5, 2.0, R) / u[:, 0]).astype(np.float32),
        "offs": striped(np.random.permutation(T)[:M]),
        "offs2": striped(np.random.permutation(T)[:J]),
    }


def reference(tab_words, tab_scales, tab2_words, tab2_scales, wa_words, wa_scales, wb, sa, sb, offs, offs2):
    idx = unstriped(offs)
    idx2 = unstriped(offs2)
    tab_ = unpack_weight(tab_words, tab_scales, "e4m3")[:, idx]
    tab2_ = unpack_weight(tab2_words, tab2_scales, "e4m3")[:, idx2]
    wa_ = unpack_weight(wa_words, wa_scales, "e2m1")
    wb_ = mxq(f64(wb), 0, "e4m3")
    za = wa_.T @ tab_
    zb = wb_.T @ tab2_
    ha = f64(sa)[:, None] * silu(za)
    hb = f64(sb)[:, None] * silu(zb)
    ha_ = mxq(ha, 0, "e4m3")
    hb_ = mxq(hb, 0, "e4m3")
    y = ha_.T @ hb_
    return y * 0.03125

@@ -1,0 +1,277 @@
+from contextlib import ExitStack
+
+import concourse.mybir as mybir
+from concourse.masks import make_identity
+
+K, R, T, M, J = 1024, 1024, 2048, 512, 1024
+FLOPS = 2 * K * R * M + 2 * K * R * J + 2 * R * M * J
+
+F32 = mybir.dt.float32
+BF16 = mybir.dt.bfloat16
+I32 = mybir.dt.int32
+U32 = mybir.dt.uint32
+U16 = mybir.dt.uint16
+U8 = mybir.dt.uint8
+FP8X4 = mybir.dt.float8_e4m3fn_x4
+FP4X4 = mybir.dt.float4_e2m1fn_x4
+ACT = mybir.ActivationFunctionType
+MULT = mybir.AluOpType.mult
+
+P = 128
+PASS = 512
+NT = 128
+OUT_SCALE = 0.03125
+
+
+def tile_list_biaff_silu_none_kernel(
+    tc, tab_words, tab_scales, tab2_words, tab2_scales, wa_words, wa_scales, wb, sa, sb, offs, offs2, out
+):
+    nc = tc.nc
+    with ExitStack() as ctx:
+        keep = ctx.enter_context(tc.tile_pool(name="keep", bufs=1))
+        ring = ctx.enter_context(tc.tile_pool(name="ring", bufs=3))
+        big = ctx.enter_context(tc.tile_pool(name="big", bufs=4))
+        zpool = ctx.enter_context(tc.psum_pool(name="zpool", bufs=5))
+        ypool = ctx.enter_context(tc.psum_pool(name="ypool", bufs=3))
+
+        def held(name, shape, dtype):
+            return keep.tile(shape, dtype, name=name, align_bytes=64)
+
+        list_a = keep.tile([P, M // 16], U16, name="list_a")
+        list_b = keep.tile([P, J // 16], U16, name="list_b")
+        tb_scale = held("tb_scale", [P, T], U8)
+        ta_scale = held("ta_scale", [P, T], U8)
+        wa_scale_raw = held("wa_scale_raw", [P, 2 * R], U8)
+
+        def streamed(shape, dtype):
+            return big.tile(shape, dtype, name="big", align_bytes=64)
+
+        wb_raw = {}
+        ta_words = {}
+        tb_words = {}
+        s_rows = held("s_rows", [P, 2 * P], F32)
+        ident = held("ident", [P, P], F32)
+        s_cols = held("s_cols", [P, 4, 1, 4], F32)
+
+        def load_wb(a, b):
+            wb_raw[a, b] = streamed([P, 4, PASS], F32)
+            rows = wb[PASS * a : PASS * (a + 1), PASS * b : PASS * (b + 1)]
+            nc.sync.dma_start(wb_raw[a, b][:], rows.rearrange("(p j) c -> p j c", j=4))
+
+        def load_words(tiles, words, a):
+            tiles[a] = streamed([P, T], I32)
+            nc.sync.dma_start(tiles[a][:], words[a].rearrange("p t i -> p (t i)").bitcast(I32))
+
+        def load_packed_scales(queue, tile, scales):
+            for q in range(4):
+                queue.dma_start(
+                    tile[32 * q : 32 * q + 8, :].bitcast(I32), scales[:, 4 * q : 4 * q + 4, :].bitcast(I32)
+                )
+
+        nc.sync.dma_start(list_b[:], offs2)
+        nc.sync.dma_start(list_a[:], offs)
+        nc.gpsimd.memset(tb_scale[:].bitcast(I32), 0)
+        nc.vector.memset(ta_scale[:].bitcast(I32), 0)
+        nc.gpsimd.memset(s_rows[:], 0.0)
+        nc.vector.memset(wa_scale_raw[:].bitcast(I32), 0)
+        ga_scale1 = held("ga_scale1", [P, M], U8)
+        nc.vector.memset(ga_scale1[:].bitcast(I32), 0)
+        load_packed_scales(nc.scalar, tb_scale, tab2_scales)
+        load_wb(0, 0)
+        load_words(tb_words, tab2_words, 0)
+        load_wb(1, 0)
+        load_words(tb_words, tab2_words, 1)
+        for v, vec in enumerate((sa, sb)):
+            nc.gpsimd.dma_start(
+                s_rows[4 * v : 4 * v + 4, :].rearrange("t (g i) -> t g i", i=8),
+                vec.rearrange("(g t i) -> t g i", t=4, i=8),
+            )
+        make_identity(nc, ident[:])
+        load_packed_scales(nc.gpsimd, ta_scale, tab_scales)
+        for q in range(4):
+            nc.gpsimd.dma_start(
+                wa_scale_raw[32 * q : 32 * q + 4, :].bitcast(I32).rearrange("r (a w) -> r a w", a=2),
+                wa_scales[:, 4 * q : 4 * q + 4, :].bitcast(I32).rearrange("a r w -> r a w"),
+            )
+        load_wb(0, 1)
+        load_wb(1, 1)
+        load_words(ta_words, tab_words, 0)
+        wa_raw = streamed([P, 2 * R // 2], I32)
+        nc.sync.dma_start(
+            wa_raw[:].rearrange("p (a w) -> p a w", a=2), wa_words.bitcast(I32).rearrange("a p w -> p a w")
+        )
+        load_words(ta_words, tab_words, 1)
+
+        gb_scale = held("gb_scale", [P, J], U8)
+        gb_words = [held(f"gb_words{a}", [P, J], U32) for a in range(2)]
+        ga_words = [held(f"ga_words{a}", [P, M], U32) for a in range(2)]
+
+        def gather(dst, window, lst, lo, hi):
+            nc.vector.tensor_copy(dst[:, lo:hi], window.indirect(lst[:, lo // 16 : hi // 16]))
+
+        wb_bf = {ab: held(f"wb_bf{ab[0]}{ab[1]}", [P, 4 * PASS], BF16) for ab in wb_raw}
+        wb_codes = {ab: held(f"wb_codes{ab[0]}{ab[1]}", [P, PASS], U32) for ab in wb_raw}
+        wb_scale = {ab: held(f"wb_scale{ab[0]}{ab[1]}", [P, PASS], U8) for ab in wb_raw}
+
+        def cast_wb(a, b):
+            nc.scalar.copy(
+                wb_bf[a, b][:].rearrange("p (t q i j) -> p t q j i", t=4, i=8, j=4),
+                wb_raw[a, b][:].rearrange("p j (q t i) -> p t q j i", t=4, i=8),
+            )
+
+        def quant_wb(a, b):
+            nc.vector.quantize_mx(out=wb_codes[a, b][:].bitcast(FP8X4), scales=wb_scale[a, b][:], in_=wb_bf[a, b][:])
+
+        gather(gb_scale, tb_scale[:], list_b, 0, J)
+        cast_wb(0, 0)
+        for h in range(2):
+            gather(gb_words[0], tb_words[0][:].bitcast(U32), list_b, 512 * h, 512 * (h + 1))
+        quant_wb(0, 0)
+        cast_wb(1, 0)
+
+        s_turned = ypool.tile([P, 2, P], F32, name="y")
+        for b in range(2):
+            nc.tensor.transpose(s_turned[:, b, :], s_rows[:, P * b : P * (b + 1)], ident[:])
+        nc.vector.tensor_copy(
+            s_cols[:].rearrange("p (v b) o t -> p v b (o t)", v=2),
+            s_turned[:, :, 0:8].rearrange("p b (v t) -> p v b t", v=2),
+        )
+
+        gather(gb_words[1], tb_words[1][:].bitcast(U32), list_b, 0, 512)
+        quant_wb(1, 0)
+        gather(gb_words[1], tb_words[1][:].bitcast(U32), list_b, 512, J)
+        ga_scale = [held("wb_bf10", [P, M], U8), ga_scale1]
+        gather(ga_scale[0], ta_scale[:], list_a, 0, M)
+        for q in range(4):
+            nc.gpsimd.dma_start(
+                ga_scale1[32 * q : 32 * q + 4, :].bitcast(I32), ga_scale[0][32 * q + 4 : 32 * q + 8, :].bitcast(I32)
+            )
+
+        def z_bank_b(b, n0, act):
+            z = zpool.tile([P, 4, NT], F32, name="z")
+            for t in range(4):
+                for a in range(2):
+                    nc.tensor.matmul_mx(
+                        z[:, t, :],
+                        lhsT=wb_codes[a, b][:, P * t : P * (t + 1)].bitcast(FP8X4),
+                        lhsT_scale=wb_scale[a, b][:, P * t : P * (t + 1)],
+                        rhs=gb_words[a][:, n0 : n0 + NT].bitcast(FP8X4),
+                        rhs_scale=gb_scale[4 * a : P, n0 : n0 + NT],
+                        start=(a == 0),
+                        stop=(a == 1),
+                    )
+            nc.scalar.activation(act, z[:].rearrange("p t n -> p n t"), ACT.Silu)
+
+        wa_codes = held("wa_codes", [P, 2 * R // 2], I32)
+        wa_scale = held("wa_scale", [P, 2 * R], U8)
+
+        def z_bank_a(b, n0, act):
+            z = zpool.tile([P, 4, NT], F32, name="z")
+            for t in range(4):
+                for a in range(2):
+                    c0 = R * a + PASS * b + P * t
+                    nc.tensor.matmul_mx(
+                        z[:, t, :],
+                        lhsT=wa_codes[:].bitcast(U8)[:, 2 * c0 : 2 * (c0 + P)].bitcast(FP4X4),
+                        lhsT_scale=wa_scale[:, c0 : c0 + P],
+                        rhs=ga_words[a][:, n0 : n0 + NT].bitcast(FP8X4),
+                        rhs_scale=ga_scale[a][:, n0 : n0 + NT],
+                        start=(a == 0),
+                        stop=(a == 1),
+                    )
+            nc.scalar.activation(act, z[:].rearrange("p t n -> p n t"), ACT.Silu)
+
+        hb_codes = [held(f"hb_codes{b}", [P, J], U32) for b in range(2)]
+        hb_scale = [held(f"hb_scale{b}", [P, J], U8) for b in range(2)]
+        ha_codes = [held(f"ha_codes{m}", [P, 2 * NT], U32) for m in range(4)]
+        ha_scale = [held(f"ha_scale{m}", [P, 2 * NT], U8) for m in range(4)]
+
+        def hidden_b(b, n0):
+            act = ring.tile([P, 2, NT, 4], F32, name="act", align_bytes=64)
+            for u in range(2):
+                z_bank_b(b, n0 + NT * u, act[:, u, :, :])
+            h = ring.tile([P, 2 * NT * 4], BF16, name="h", align_bytes=64)
+            nc.vector.tensor_tensor(
+                h[:].rearrange("p (n t) -> p n t", t=4),
+                act[:].rearrange("p u n t -> p (u n) t"),
+                s_cols[:, 2 + b, :, :].to_broadcast([P, 2 * NT, 4]),
+                MULT,
+            )
+            return h, hb_codes[b][:, n0 : n0 + 2 * NT], hb_scale[b][:, n0 : n0 + 2 * NT]
+
+        def hidden_a(m):
+            act = ring.tile([P, 2, NT, 4], F32, name="act", align_bytes=64)
+            for b in range(2):
+                z_bank_a(b, NT * m, act[:, b, :, :])
+            h = ring.tile([P, 2 * NT * 4], BF16, name="h", align_bytes=64)
+            nc.vector.tensor_tensor(
+                h[:].rearrange("p (b n t) -> p b n t", b=2, t=4),
+                act[:],
+                s_cols[:, 0:2, :, :].to_broadcast([P, 2, NT, 4]),
+                MULT,
+            )
+            return h, ha_codes[m][:], ha_scale[m][:]
+
+        def quant_h(h, codes, scale):
+            nc.vector.quantize_mx(out=codes.bitcast(FP8X4), scales=scale, in_=h[:])
+
+        def scores(m):
+            res = ring.tile([P, J], F32, name="res", bufs=4)
+            for jh in range(2):
+                cols = slice(512 * jh, 512 * (jh + 1))
+                y = ypool.tile([P, 512], F32, name="y")
+                for b in range(2):
+                    nc.tensor.matmul_mx(
+                        y[:],
+                        lhsT=ha_codes[m][:, NT * b : NT * (b + 1)].bitcast(FP8X4),
+                        lhsT_scale=ha_scale[m][:, NT * b : NT * (b + 1)],
+                        rhs=hb_codes[b][:, cols].bitcast(FP8X4),
+                        rhs_scale=hb_scale[b][:, cols],
+                        start=(b == 0),
+                        stop=(b == 1),
+                    )
+                if m == 3 and jh == 1:
+                    nc.vector.tensor_scalar_mul(res[:, cols], y[:], OUT_SCALE)
+                else:
+                    nc.scalar.activation(res[:, cols], y[:], ACT.Copy, scale=OUT_SCALE)
+                nc.sync.dma_start(out[NT * m : NT * (m + 1), cols], res[:, cols])
+
+        def prepare_a(step):
+            if step == 1:
+                nc.vector.tensor_copy(
+                    wa_scale[:].bitcast(I32).rearrange("p (g t q w) -> p g t q w", t=4, q=16, w=2),
+                    wa_scale_raw[:].bitcast(I32).rearrange("p (g q t w) -> p g t q w", t=4, q=16, w=2),
+                )
+                gather(ga_words[0], ta_words[0][:].bitcast(U32), list_a, 0, M)
+            if step == 2:
+                nc.vector.tensor_copy(
+                    wa_codes[:].rearrange("p (g t q w) -> p g t q w", t=4, q=16, w=4),
+                    wa_raw[:].rearrange("p (g q t w) -> p g t q w", t=4, q=16, w=4),
+                )
+            if step == 3:
+                for h in range(2):
+                    gather(ga_words[1], ta_words[1][:].bitcast(U32), list_a, 256 * h, 256 * (h + 1))
+
+        pending = None
+        for i in range(8):
+            b, n0 = i // 4, 256 * (i % 4)
+            made = hidden_b(b, n0)
+            if pending is not None:
+                quant_h(*pending)
+            pending = made
+            if i == 0:
+                cast_wb(0, 1)
+                quant_wb(0, 1)
+            if i == 1:
+                cast_wb(1, 1)
+                quant_wb(1, 1)
+            if i >= 4:
+                prepare_a(i - 4)
+        for m in range(4):
+            made = hidden_a(m)
+            quant_h(*pending)
+            pending = made
+            if m > 0:
+                scores(m - 1)
+        quant_h(*pending)
+        scores(3)

@@ -29,7 +29,7 @@ def tile_list_biaff_silu_none_kernel(
     nc = tc.nc
     with ExitStack() as ctx:
         keep = ctx.enter_context(tc.tile_pool(name="keep", bufs=1))
-        ring = ctx.enter_context(tc.tile_pool(name="ring", bufs=3))
+        ring = ctx.enter_context(tc.tile_pool(name="ring", bufs=4))
         big = ctx.enter_context(tc.tile_pool(name="big", bufs=4))
         zpool = ctx.enter_context(tc.psum_pool(name="zpool", bufs=5))
         ypool = ctx.enter_context(tc.psum_pool(name="ypool", bufs=3))
@@ -41,7 +41,6 @@ def tile_list_biaff_silu_none_kernel(
         list_b = keep.tile([P, J // 16], U16, name="list_b")
         tb_scale = held("tb_scale", [P, T], U8)
         ta_scale = held("ta_scale", [P, T], U8)
-        wa_scale_raw = held("wa_scale_raw", [P, 2 * R], U8)
 
         def streamed(shape, dtype):
             return big.tile(shape, dtype, name="big", align_bytes=64)
@@ -62,37 +61,37 @@ def tile_list_biaff_silu_none_kernel(
             tiles[a] = streamed([P, T], I32)
             nc.sync.dma_start(tiles[a][:], words[a].rearrange("p t i -> p (t i)").bitcast(I32))
 
-        def load_packed_scales(queue, tile, scales):
+        def load_scale_rows(tile, scales):
+            nc.sync.dma_start(tile[96:P, :].bitcast(I32), scales.bitcast(I32).rearrange("a q w -> q a w"))
+
+        def place_scale_rows(queue, plane, picked):
             for q in range(4):
                 queue.dma_start(
-                    tile[32 * q : 32 * q + 8, :].bitcast(I32), scales[:, 4 * q : 4 * q + 4, :].bitcast(I32)
+                    plane[32 * q : 32 * q + 4, :].bitcast(I32), picked[96 + 8 * q : 96 + 8 * q + 8, :].bitcast(I32)
                 )
 
+        gb_scale = held("gb_scale", [P, 2 * J], U8)
+        warm = held("warm", [P, 2], F32)
         nc.sync.dma_start(list_b[:], offs2)
+        load_scale_rows(tb_scale, tab2_scales)
         nc.sync.dma_start(list_a[:], offs)
-        nc.gpsimd.memset(tb_scale[:].bitcast(I32), 0)
-        nc.vector.memset(ta_scale[:].bitcast(I32), 0)
+        load_scale_rows(ta_scale, tab_scales)
+        nc.vector.memset(tb_scale[0:96, :].bitcast(I32), 0)
+        nc.vector.memset(gb_scale[:].bitcast(I32), 0)
+        nc.vector.memset(ta_scale[0:96, :].bitcast(I32), 0)
+        nc.gpsimd.memset(warm[:], 0.0)
+        nc.scalar.activation(warm[:, 0:1], warm[:, 1:2], ACT.Silu)
         nc.gpsimd.memset(s_rows[:], 0.0)
-        nc.vector.memset(wa_scale_raw[:].bitcast(I32), 0)
-        ga_scale1 = held("ga_scale1", [P, M], U8)
-        nc.vector.memset(ga_scale1[:].bitcast(I32), 0)
-        load_packed_scales(nc.scalar, tb_scale, tab2_scales)
         load_wb(0, 0)
         load_words(tb_words, tab2_words, 0)
         load_wb(1, 0)
         load_words(tb_words, tab2_words, 1)
         for v, vec in enumerate((sa, sb)):
-            nc.gpsimd.dma_start(
+            nc.scalar.dma_start(
                 s_rows[4 * v : 4 * v + 4, :].rearrange("t (g i) -> t g i", i=8),
                 vec.rearrange("(g t i) -> t g i", t=4, i=8),
             )
         make_identity(nc, ident[:])
-        load_packed_scales(nc.gpsimd, ta_scale, tab_scales)
-        for q in range(4):
-            nc.gpsimd.dma_start(
-                wa_scale_raw[32 * q : 32 * q + 4, :].bitcast(I32).rearrange("r (a w) -> r a w", a=2),
-                wa_scales[:, 4 * q : 4 * q + 4, :].bitcast(I32).rearrange("a r w -> r a w"),
-            )
         load_wb(0, 1)
         load_wb(1, 1)
         load_words(ta_words, tab_words, 0)
@@ -102,118 +101,138 @@ def tile_list_biaff_silu_none_kernel(
         )
         load_words(ta_words, tab_words, 1)
 
-        gb_scale = held("gb_scale", [P, J], U8)
+        gb_picked = held("gb_picked", [P, J], U8)
         gb_words = [held(f"gb_words{a}", [P, J], U32) for a in range(2)]
-        ga_words = [held(f"ga_words{a}", [P, M], U32) for a in range(2)]
+        ga_words = {}
 
         def gather(dst, window, lst, lo, hi):
             nc.vector.tensor_copy(dst[:, lo:hi], window.indirect(lst[:, lo // 16 : hi // 16]))
 
-        wb_bf = {ab: held(f"wb_bf{ab[0]}{ab[1]}", [P, 4 * PASS], BF16) for ab in wb_raw}
+        wb_bf = {}
         wb_codes = {ab: held(f"wb_codes{ab[0]}{ab[1]}", [P, PASS], U32) for ab in wb_raw}
         wb_scale = {ab: held(f"wb_scale{ab[0]}{ab[1]}", [P, PASS], U8) for ab in wb_raw}
 
         def cast_wb(a, b):
-            nc.scalar.copy(
-                wb_bf[a, b][:].rearrange("p (t q i j) -> p t q j i", t=4, i=8, j=4),
-                wb_raw[a, b][:].rearrange("p j (q t i) -> p t q j i", t=4, i=8),
-            )
+            wb_bf[a, b] = held(f"wb_bf{a}0" if b == 0 else f"act{a}", [P, 4 * PASS], BF16)
+            dst = wb_bf[a, b][:].rearrange("p (t q u i j) -> p t q u j i", t=4, u=2, i=4, j=4)
+            src = wb_raw[a, b][:].rearrange("p j (q t u i) -> p t q u j i", t=4, u=2, i=4)
+            for t in range(4):
+                nc.scalar.copy(dst[:, t], src[:, t])
 
         def quant_wb(a, b):
             nc.vector.quantize_mx(out=wb_codes[a, b][:].bitcast(FP8X4), scales=wb_scale[a, b][:], in_=wb_bf[a, b][:])
 
-        gather(gb_scale, tb_scale[:], list_b, 0, J)
+        gather(gb_picked, tb_scale[:], list_b, 0, J)
         cast_wb(0, 0)
+        place_scale_rows(nc.scalar, gb_scale, gb_picked)
         for h in range(2):
             gather(gb_words[0], tb_words[0][:].bitcast(U32), list_b, 512 * h, 512 * (h + 1))
         quant_wb(0, 0)
+        wa_scale_raw = held("wb_bf00", [P, 2 * R], U8)
+        nc.vector.memset(wa_scale_raw[:].bitcast(I32), 0)
+        for q in range(4):
+            nc.sync.dma_start(
+                wa_scale_raw[32 * q : 32 * q + 4, :].bitcast(I32).rearrange("r (a w) -> r a w", a=2),
+                wa_scales[:, 4 * q : 4 * q + 4, :].bitcast(I32).rearrange("a r w -> r a w"),
+            )
         cast_wb(1, 0)
 
         s_turned = ypool.tile([P, 2, P], F32, name="y")
         for b in range(2):
             nc.tensor.transpose(s_turned[:, b, :], s_rows[:, P * b : P * (b + 1)], ident[:])
-        nc.vector.tensor_copy(
+        nc.scalar.copy(
             s_cols[:].rearrange("p (v b) o t -> p v b (o t)", v=2),
             s_turned[:, :, 0:8].rearrange("p b (v t) -> p v b t", v=2),
         )
 
-        gather(gb_words[1], tb_words[1][:].bitcast(U32), list_b, 0, 512)
         quant_wb(1, 0)
-        gather(gb_words[1], tb_words[1][:].bitcast(U32), list_b, 512, J)
-        ga_scale = [held("wb_bf10", [P, M], U8), ga_scale1]
-        gather(ga_scale[0], ta_scale[:], list_a, 0, M)
-        for q in range(4):
-            nc.gpsimd.dma_start(
-                ga_scale1[32 * q : 32 * q + 4, :].bitcast(I32), ga_scale[0][32 * q + 4 : 32 * q + 8, :].bitcast(I32)
-            )
+        for lo, hi in ((0, 256), (256, 512), (512, J)):
+            gather(gb_words[1], tb_words[1][:].bitcast(U32), list_b, lo, hi)
+        ga_picked = held("ga_picked", [P, M], U8)
+        gather(ga_picked, ta_scale[:], list_a, 0, M)
+        ga_scale = held("wb_bf10", [P, 2 * M], U8)
+        nc.vector.memset(ga_scale[:].bitcast(I32), 0)
+        place_scale_rows(nc.sync, ga_scale, ga_picked)
 
-        def z_bank_b(b, n0, act):
-            z = zpool.tile([P, 4, NT], F32, name="z")
+        wa = {}
+
+        def z_passes(z, i, u, a):
             for t in range(4):
-                for a in range(2):
-                    nc.tensor.matmul_mx(
-                        z[:, t, :],
-                        lhsT=wb_codes[a, b][:, P * t : P * (t + 1)].bitcast(FP8X4),
-                        lhsT_scale=wb_scale[a, b][:, P * t : P * (t + 1)],
-                        rhs=gb_words[a][:, n0 : n0 + NT].bitcast(FP8X4),
-                        rhs_scale=gb_scale[4 * a : P, n0 : n0 + NT],
-                        start=(a == 0),
-                        stop=(a == 1),
-                    )
-            nc.scalar.activation(act, z[:].rearrange("p t n -> p n t"), ACT.Silu)
-
-        wa_codes = held("wa_codes", [P, 2 * R // 2], I32)
-        wa_scale = held("wa_scale", [P, 2 * R], U8)
-
-        def z_bank_a(b, n0, act):
-            z = zpool.tile([P, 4, NT], F32, name="z")
-            for t in range(4):
-                for a in range(2):
-                    c0 = R * a + PASS * b + P * t
-                    nc.tensor.matmul_mx(
-                        z[:, t, :],
-                        lhsT=wa_codes[:].bitcast(U8)[:, 2 * c0 : 2 * (c0 + P)].bitcast(FP4X4),
-                        lhsT_scale=wa_scale[:, c0 : c0 + P],
-                        rhs=ga_words[a][:, n0 : n0 + NT].bitcast(FP8X4),
-                        rhs_scale=ga_scale[a][:, n0 : n0 + NT],
-                        start=(a == 0),
-                        stop=(a == 1),
-                    )
-            nc.scalar.activation(act, z[:].rearrange("p t n -> p n t"), ACT.Silu)
+                if i < 8:
+                    b, n0 = i // 4, 256 * (i % 4) + NT * u
+                    codes = wb_codes[a, b][:, P * t : P * (t + 1)].bitcast(FP8X4)
+                    scale = wb_scale[a, b][:, P * t : P * (t + 1)]
+                    moving = gb_words[a][:, n0 : n0 + NT]
+                    moving_scale = gb_scale[:, J * a + n0 : J * a + n0 + NT]
+                else:
+                    c0, n0 = R * a + PASS * u + P * t, NT * (i - 8)
+                    codes = wa["codes"][:].bitcast(U8)[:, 2 * c0 : 2 * (c0 + P)].bitcast(FP4X4)
+                    scale = wa["scale"][:, c0 : c0 + P]
+                    moving = ga_words[a][:, n0 : n0 + NT]
+                    moving_scale = ga_scale[:, M * a + n0 : M * a + n0 + NT]
+                nc.tensor.matmul_mx(
+                    z[:, t, :],
+                    lhsT=codes,
+                    lhsT_scale=scale,
+                    rhs=moving.bitcast(FP8X4),
+                    rhs_scale=moving_scale,
+                    start=(a == 0 and t == 0),
+                    stop=(a == 1 and t == 3),
+                )
 
         hb_codes = [held(f"hb_codes{b}", [P, J], U32) for b in range(2)]
         hb_scale = [held(f"hb_scale{b}", [P, J], U8) for b in range(2)]
         ha_codes = [held(f"ha_codes{m}", [P, 2 * NT], U32) for m in range(4)]
         ha_scale = [held(f"ha_scale{m}", [P, 2 * NT], U8) for m in range(4)]
 
-        def hidden_b(b, n0):
-            act = ring.tile([P, 2, NT, 4], F32, name="act", align_bytes=64)
-            for u in range(2):
-                z_bank_b(b, n0 + NT * u, act[:, u, :, :])
-            h = ring.tile([P, 2 * NT * 4], BF16, name="h", align_bytes=64)
-            nc.vector.tensor_tensor(
-                h[:].rearrange("p (n t) -> p n t", t=4),
-                act[:].rearrange("p u n t -> p (u n) t"),
-                s_cols[:, 2 + b, :, :].to_broadcast([P, 2 * NT, 4]),
-                MULT,
-            )
-            return h, hb_codes[b][:, n0 : n0 + 2 * NT], hb_scale[b][:, n0 : n0 + 2 * NT]
+        act = {}
+        h = {}
 
-        def hidden_a(m):
-            act = ring.tile([P, 2, NT, 4], F32, name="act", align_bytes=64)
-            for b in range(2):
-                z_bank_a(b, NT * m, act[:, b, :, :])
-            h = ring.tile([P, 2 * NT * 4], BF16, name="h", align_bytes=64)
-            nc.vector.tensor_tensor(
-                h[:].rearrange("p (b n t) -> p b n t", b=2, t=4),
-                act[:],
-                s_cols[:, 0:2, :, :].to_broadcast([P, 2, NT, 4]),
-                MULT,
-            )
-            return h, ha_codes[m][:], ha_scale[m][:]
+        def front(units):
+            z = {}
+            for i in units:
+                if i < 4:
+                    act[i] = held(f"act{i}", [P, 2, NT, 4], F32)
+                else:
+                    act[i] = ring.tile([P, 2, NT, 4], F32, name="act", align_bytes=64)
+                for u in range(2):
+                    z[i, u] = zpool.tile([P, 4, NT], F32, name="z")
+                    z_passes(z[i, u], i, u, 0)
+                    if len(units) == 1:
+                        z_passes(z[i, u], i, u, 1)
+                        nc.scalar.activation(act[i][:, u, :, :], z[i, u][:].rearrange("p t n -> p n t"), ACT.Silu)
+            if len(units) > 1:
+                for i, u in z:
+                    z_passes(z[i, u], i, u, 1)
+                    nc.scalar.activation(act[i][:, u, :, :], z[i, u][:].rearrange("p t n -> p n t"), ACT.Silu)
 
-        def quant_h(h, codes, scale):
-            nc.vector.quantize_mx(out=codes.bitcast(FP8X4), scales=scale, in_=h[:])
+        def back(i):
+            if i < 4:
+                h[i] = held(f"h{i}", [P, 2 * NT * 4], BF16)
+            else:
+                h[i] = ring.tile([P, 2 * NT * 4], BF16, name="h", align_bytes=64)
+            if i < 8:
+                nc.vector.tensor_tensor(
+                    h[i][:].rearrange("p (n t) -> p n t", t=4),
+                    act[i][:].rearrange("p u n t -> p (u n) t"),
+                    s_cols[:, 2 + i // 4, :, :].to_broadcast([P, 2 * NT, 4]),
+                    MULT,
+                )
+            else:
+                nc.vector.tensor_tensor(
+                    h[i][:].rearrange("p (b n t) -> p b n t", b=2, t=4),
+                    act[i][:],
+                    s_cols[:, 0:2, :, :].to_broadcast([P, 2, NT, 4]),
+                    MULT,
+                )
+
+        def quant_h(i):
+            if i < 8:
+                cols = slice(256 * (i % 4), 256 * (i % 4 + 1))
+                codes, scale = hb_codes[i // 4][:, cols], hb_scale[i // 4][:, cols]
+            else:
+                codes, scale = ha_codes[i - 8][:], ha_scale[i - 8][:]
+            nc.vector.quantize_mx(out=codes.bitcast(FP8X4), scales=scale, in_=h[i][:])
 
         def scores(m):
             res = ring.tile([P, J], F32, name="res", bufs=4)
@@ -236,42 +255,55 @@ def tile_list_biaff_silu_none_kernel(
                     nc.scalar.activation(res[:, cols], y[:], ACT.Copy, scale=OUT_SCALE)
                 nc.sync.dma_start(out[NT * m : NT * (m + 1), cols], res[:, cols])
 
-        def prepare_a(step):
-            if step == 1:
-                nc.vector.tensor_copy(
-                    wa_scale[:].bitcast(I32).rearrange("p (g t q w) -> p g t q w", t=4, q=16, w=2),
-                    wa_scale_raw[:].bitcast(I32).rearrange("p (g q t w) -> p g t q w", t=4, q=16, w=2),
-                )
-                gather(ga_words[0], ta_words[0][:].bitcast(U32), list_a, 0, M)
-            if step == 2:
-                nc.vector.tensor_copy(
-                    wa_codes[:].rearrange("p (g t q w) -> p g t q w", t=4, q=16, w=4),
-                    wa_raw[:].rearrange("p (g q t w) -> p g t q w", t=4, q=16, w=4),
-                )
-            if step == 3:
-                for h in range(2):
-                    gather(ga_words[1], ta_words[1][:].bitcast(U32), list_a, 256 * h, 256 * (h + 1))
+        def order_wa_scale():
+            wa["scale"] = held("h0", [P, 2 * R], U8)
+            nc.vector.tensor_copy(
+                wa["scale"][:].bitcast(I32).rearrange("p (g t q w) -> p g t q w", t=4, q=16, w=2),
+                wa_scale_raw[:].bitcast(I32).rearrange("p (g q t w) -> p g t q w", t=4, q=16, w=2),
+            )
 
-        pending = None
-        for i in range(8):
-            b, n0 = i // 4, 256 * (i % 4)
-            made = hidden_b(b, n0)
-            if pending is not None:
-                quant_h(*pending)
-            pending = made
-            if i == 0:
-                cast_wb(0, 1)
-                quant_wb(0, 1)
-            if i == 1:
-                cast_wb(1, 1)
-                quant_wb(1, 1)
-            if i >= 4:
-                prepare_a(i - 4)
-        for m in range(4):
-            made = hidden_a(m)
-            quant_h(*pending)
-            pending = made
-            if m > 0:
-                scores(m - 1)
-        quant_h(*pending)
+        def order_wa_codes():
+            wa["codes"] = held("act2", [P, 2 * R // 2], I32)
+            nc.vector.tensor_copy(
+                wa["codes"][:].rearrange("p (g t q w) -> p g t q w", t=4, q=16, w=4),
+                wa_raw[:].rearrange("p (g q t w) -> p g t q w", t=4, q=16, w=4),
+            )
+
+        def gather_a(a):
+            ga_words[a] = held(f"h{1 + 2 * a}", [P, M], U32)
+            gather(ga_words[a], ta_words[a][:].bitcast(U32), list_a, 0, M)
+
+        front([0, 1])
+        back(0)
+        cast_wb(0, 1)
+        back(1)
+        quant_h(0)
+        front([2])
+        quant_h(1)
+        order_wa_scale()
+        gather_a(0)
+        quant_wb(0, 1)
+        cast_wb(1, 1)
+        back(2)
+        front([3])
+        order_wa_codes()
+        quant_h(2)
+        quant_wb(1, 1)
+        front([4])
+        back(3)
+        front([5])
+        quant_h(3)
+        gather_a(1)
+        for i in range(4, 11):
+            back(i)
+            if i + 2 < 12:
+                front([i + 2])
+            if i > 4:
+                quant_h(i - 1)
+            if i > 8:
+                scores(i - 9)
+        quant_h(10)
+        scores(2)
+        back(11)
+        quant_h(11)
         scores(3)

@@ -39,16 +39,15 @@ def tile_list_biaff_silu_none_kernel(
 
         list_a = keep.tile([P, M // 16], U16, name="list_a")
         list_b = keep.tile([P, J // 16], U16, name="list_b")
-        tb_scale = held("tb_scale", [P, T], U8)
         ta_scale = held("ta_scale", [P, T], U8)
 
         def streamed(shape, dtype):
             return big.tile(shape, dtype, name="big", align_bytes=64)
 
+        tb_scale = streamed([P, T], U8)
         wb_raw = {}
         ta_words = {}
         tb_words = {}
-        s_rows = held("s_rows", [P, 2 * P], F32)
         ident = held("ident", [P, P], F32)
         s_cols = held("s_cols", [P, 4, 1, 4], F32)
 
@@ -62,7 +61,7 @@ def tile_list_biaff_silu_none_kernel(
             nc.sync.dma_start(tiles[a][:], words[a].rearrange("p t i -> p (t i)").bitcast(I32))
 
         def load_scale_rows(tile, scales):
-            nc.sync.dma_start(tile[96:P, :].bitcast(I32), scales.bitcast(I32).rearrange("a q w -> q a w"))
+            nc.scalar.dma_start(tile[96:P, :].bitcast(I32), scales.bitcast(I32).rearrange("a q w -> q a w"))
 
         def place_scale_rows(queue, plane, picked):
             for q in range(4):
@@ -72,34 +71,35 @@ def tile_list_biaff_silu_none_kernel(
 
         gb_scale = held("gb_scale", [P, 2 * J], U8)
         warm = held("warm", [P, 2], F32)
+
+        def load_factor(queue, buf, vec):
+            rows = held(buf, [P, 2 * P], F32)
+            nc.gpsimd.memset(rows[:], 0.0)
+            queue.dma_start(
+                rows[0:4, :].rearrange("t (g i) -> t g i", i=8), vec.rearrange("(g t i) -> t g i", t=4, i=8)
+            )
+            return rows
+
+        def turn_factor(rows, v):
+            turned = ypool.tile([P, 2, P], F32, name="y")
+            for b in range(2):
+                nc.tensor.transpose(turned[:, b, :], rows[:, P * b : P * (b + 1)], ident[:])
+            nc.scalar.copy(s_cols[:, 2 * v : 2 * v + 2, 0, :], turned[:, :, 0:4])
+
         nc.sync.dma_start(list_b[:], offs2)
         load_scale_rows(tb_scale, tab2_scales)
-        nc.sync.dma_start(list_a[:], offs)
         load_scale_rows(ta_scale, tab_scales)
         nc.vector.memset(tb_scale[0:96, :].bitcast(I32), 0)
         nc.vector.memset(gb_scale[:].bitcast(I32), 0)
         nc.vector.memset(ta_scale[0:96, :].bitcast(I32), 0)
         nc.gpsimd.memset(warm[:], 0.0)
-        nc.scalar.activation(warm[:, 0:1], warm[:, 1:2], ACT.Silu)
-        nc.gpsimd.memset(s_rows[:], 0.0)
+        nc.sync.dma_start(list_a[:], offs)
         load_wb(0, 0)
         load_words(tb_words, tab2_words, 0)
         load_wb(1, 0)
-        load_words(tb_words, tab2_words, 1)
-        for v, vec in enumerate((sa, sb)):
-            nc.scalar.dma_start(
-                s_rows[4 * v : 4 * v + 4, :].rearrange("t (g i) -> t g i", i=8),
-                vec.rearrange("(g t i) -> t g i", t=4, i=8),
-            )
+        sb_rows = load_factor(nc.scalar, "sb_rows", sb)
+        nc.scalar.activation(warm[:, 0:1], warm[:, 1:2], ACT.Silu)
         make_identity(nc, ident[:])
-        load_wb(0, 1)
-        load_wb(1, 1)
-        load_words(ta_words, tab_words, 0)
-        wa_raw = streamed([P, 2 * R // 2], I32)
-        nc.sync.dma_start(
-            wa_raw[:].rearrange("p (a w) -> p a w", a=2), wa_words.bitcast(I32).rearrange("a p w -> p a w")
-        )
-        load_words(ta_words, tab_words, 1)
 
         gb_picked = held("gb_picked", [P, J], U8)
         gb_words = [held(f"gb_words{a}", [P, J], U32) for a in range(2)]
@@ -109,67 +109,67 @@ def tile_list_biaff_silu_none_kernel(
             nc.vector.tensor_copy(dst[:, lo:hi], window.indirect(lst[:, lo // 16 : hi // 16]))
 
         wb_bf = {}
-        wb_codes = {ab: held(f"wb_codes{ab[0]}{ab[1]}", [P, PASS], U32) for ab in wb_raw}
-        wb_scale = {ab: held(f"wb_scale{ab[0]}{ab[1]}", [P, PASS], U8) for ab in wb_raw}
+        wb_codes = {(a, b): held(f"wb_codes{a}{b}", [P, PASS], U32) for a in range(2) for b in range(2)}
+        wb_scale = {(a, b): held(f"wb_scale{a}{b}", [P, PASS], U8) for a in range(2) for b in range(2)}
 
-        def cast_wb(a, b):
+        def cast_wb(a, b, on_vector=0):
             wb_bf[a, b] = held(f"wb_bf{a}0" if b == 0 else f"act{a}", [P, 4 * PASS], BF16)
-            dst = wb_bf[a, b][:].rearrange("p (t q u i j) -> p t q u j i", t=4, u=2, i=4, j=4)
-            src = wb_raw[a, b][:].rearrange("p j (q t u i) -> p t q u j i", t=4, u=2, i=4)
+            dst = wb_bf[a, b][:].rearrange("p (t q u i j) -> p t q u j i", t=4, u=4, i=2, j=4)
+            src = wb_raw[a, b][:].rearrange("p j (q t u i) -> p t q u j i", t=4, u=4, i=2)
             for t in range(4):
-                nc.scalar.copy(dst[:, t], src[:, t])
+                if t < 4 - on_vector:
+                    nc.scalar.copy(dst[:, t], src[:, t])
+                else:
+                    nc.vector.tensor_copy(dst[:, t], src[:, t])
 
         def quant_wb(a, b):
             nc.vector.quantize_mx(out=wb_codes[a, b][:].bitcast(FP8X4), scales=wb_scale[a, b][:], in_=wb_bf[a, b][:])
 
         gather(gb_picked, tb_scale[:], list_b, 0, J)
+        place_scale_rows(nc.sync, gb_scale, gb_picked)
+        load_words(tb_words, tab2_words, 1)
         cast_wb(0, 0)
-        place_scale_rows(nc.scalar, gb_scale, gb_picked)
+        load_wb(0, 1)
         for h in range(2):
             gather(gb_words[0], tb_words[0][:].bitcast(U32), list_b, 512 * h, 512 * (h + 1))
+        load_wb(1, 1)
         quant_wb(0, 0)
         wa_scale_raw = held("wb_bf00", [P, 2 * R], U8)
-        nc.vector.memset(wa_scale_raw[:].bitcast(I32), 0)
+        nc.gpsimd.memset(wa_scale_raw[:].bitcast(I32), 0)
         for q in range(4):
             nc.sync.dma_start(
                 wa_scale_raw[32 * q : 32 * q + 4, :].bitcast(I32).rearrange("r (a w) -> r a w", a=2),
                 wa_scales[:, 4 * q : 4 * q + 4, :].bitcast(I32).rearrange("a r w -> r a w"),
             )
-        cast_wb(1, 0)
-
-        s_turned = ypool.tile([P, 2, P], F32, name="y")
-        for b in range(2):
-            nc.tensor.transpose(s_turned[:, b, :], s_rows[:, P * b : P * (b + 1)], ident[:])
-        nc.scalar.copy(
-            s_cols[:].rearrange("p (v b) o t -> p v b (o t)", v=2),
-            s_turned[:, :, 0:8].rearrange("p b (v t) -> p v b t", v=2),
-        )
-
+        ga_picked = held("ga_picked", [P, M], U8)
+        gather(ga_picked, ta_scale[:], list_a, 0, M)
+        cast_wb(1, 0, on_vector=2)
+        load_words(ta_words, tab_words, 0)
+        turn_factor(sb_rows, 1)
         quant_wb(1, 0)
         for lo, hi in ((0, 256), (256, 512), (512, J)):
             gather(gb_words[1], tb_words[1][:].bitcast(U32), list_b, lo, hi)
-        ga_picked = held("ga_picked", [P, M], U8)
-        gather(ga_picked, ta_scale[:], list_a, 0, M)
-        ga_scale = held("wb_bf10", [P, 2 * M], U8)
-        nc.vector.memset(ga_scale[:].bitcast(I32), 0)
-        place_scale_rows(nc.sync, ga_scale, ga_picked)
+        wa_raw = streamed([P, 2 * R // 2], I32)
+        nc.sync.dma_start(
+            wa_raw[:].rearrange("p (a w) -> p a w", a=2), wa_words.bitcast(I32).rearrange("a p w -> p a w")
+        )
+        load_words(ta_words, tab_words, 1)
 
         wa = {}
 
-        def z_passes(z, i, u, a):
+        def z_passes(z, side, b, n0, a):
             for t in range(4):
-                if i < 8:
-                    b, n0 = i // 4, 256 * (i % 4) + NT * u
+                if side == "b":
                     codes = wb_codes[a, b][:, P * t : P * (t + 1)].bitcast(FP8X4)
                     scale = wb_scale[a, b][:, P * t : P * (t + 1)]
                     moving = gb_words[a][:, n0 : n0 + NT]
                     moving_scale = gb_scale[:, J * a + n0 : J * a + n0 + NT]
                 else:
-                    c0, n0 = R * a + PASS * u + P * t, NT * (i - 8)
+                    c0 = R * a + PASS * b + P * t
                     codes = wa["codes"][:].bitcast(U8)[:, 2 * c0 : 2 * (c0 + P)].bitcast(FP4X4)
                     scale = wa["scale"][:, c0 : c0 + P]
                     moving = ga_words[a][:, n0 : n0 + NT]
-                    moving_scale = ga_scale[:, M * a + n0 : M * a + n0 + NT]
+                    moving_scale = wa["tab_scale"][:, M * a + n0 : M * a + n0 + NT]
                 nc.tensor.matmul_mx(
                     z[:, t, :],
                     lhsT=codes,
@@ -185,78 +185,102 @@ def tile_list_biaff_silu_none_kernel(
         ha_codes = [held(f"ha_codes{m}", [P, 2 * NT], U32) for m in range(4)]
         ha_scale = [held(f"ha_scale{m}", [P, 2 * NT], U8) for m in range(4)]
 
+        units = [("b", [(0, NT * (2 * i + u)) for u in range(2)]) for i in range(4)]
+        units = units + [("b", [(1, NT * (4 * i + u)) for u in range(4)]) for i in range(2)]
+        units = units + [("a", [(b, NT * m) for b in range(2)]) for m in range(3)]
+        units = units + [("a", [(b, NT * 3)]) for b in range(2)]
         act = {}
         h = {}
 
-        def front(units):
+        def silu(z, i, u):
+            nc.scalar.activation(act[i][:, u, :, :], z[:].rearrange("p t n -> p n t"), ACT.Silu)
+
+        def act_tile(i):
+            shape = [P, len(units[i][1]), NT, 4]
+            if i < 4:
+                return held(f"act{i}", shape, F32)
+            return ring.tile(shape, F32, name="act", align_bytes=64)
+
+        def front(i):
+            side, banks = units[i]
+            act[i] = act_tile(i)
+            for u, (b, n0) in enumerate(banks):
+                z = zpool.tile([P, 4, NT], F32, name="z")
+                for a in range(2):
+                    z_passes(z, side, b, n0, a)
+                silu(z, i, u)
+
+        def first_fronts():
             z = {}
-            for i in units:
-                if i < 4:
-                    act[i] = held(f"act{i}", [P, 2, NT, 4], F32)
-                else:
-                    act[i] = ring.tile([P, 2, NT, 4], F32, name="act", align_bytes=64)
-                for u in range(2):
+            for i in range(2):
+                act[i] = act_tile(i)
+                for u, (b, n0) in enumerate(units[i][1]):
                     z[i, u] = zpool.tile([P, 4, NT], F32, name="z")
-                    z_passes(z[i, u], i, u, 0)
-                    if len(units) == 1:
-                        z_passes(z[i, u], i, u, 1)
-                        nc.scalar.activation(act[i][:, u, :, :], z[i, u][:].rearrange("p t n -> p n t"), ACT.Silu)
-            if len(units) > 1:
-                for i, u in z:
-                    z_passes(z[i, u], i, u, 1)
-                    nc.scalar.activation(act[i][:, u, :, :], z[i, u][:].rearrange("p t n -> p n t"), ACT.Silu)
+                    z_passes(z[i, u], "b", b, n0, 0)
+            for i, u in z:
+                b, n0 = units[i][1][u]
+                z_passes(z[i, u], "b", b, n0, 1)
+                silu(z[i, u], i, u)
 
         def back(i):
+            side, banks = units[i]
+            shape = [P, len(banks), NT, 4]
             if i < 4:
-                h[i] = held(f"h{i}", [P, 2 * NT * 4], BF16)
+                h[i] = held(f"h{i}", shape, BF16)
             else:
-                h[i] = ring.tile([P, 2 * NT * 4], BF16, name="h", align_bytes=64)
-            if i < 8:
+                h[i] = ring.tile(shape, BF16, name="h", align_bytes=64)
+            b0 = banks[0][0]
+            if side == "b":
+                factor = s_cols[:, 2 + b0, :, :].to_broadcast([P, len(banks) * NT, 4])
                 nc.vector.tensor_tensor(
-                    h[i][:].rearrange("p (n t) -> p n t", t=4),
-                    act[i][:].rearrange("p u n t -> p (u n) t"),
-                    s_cols[:, 2 + i // 4, :, :].to_broadcast([P, 2 * NT, 4]),
-                    MULT,
+                    h[i][:].rearrange("p u n t -> p (u n) t"), act[i][:].rearrange("p u n t -> p (u n) t"), factor, MULT
                 )
             else:
-                nc.vector.tensor_tensor(
-                    h[i][:].rearrange("p (b n t) -> p b n t", b=2, t=4),
-                    act[i][:],
-                    s_cols[:, 0:2, :, :].to_broadcast([P, 2, NT, 4]),
-                    MULT,
-                )
+                factor = s_cols[:, b0 : b0 + len(banks), :, :].to_broadcast(shape)
+                nc.vector.tensor_tensor(h[i][:], act[i][:], factor, MULT)
 
         def quant_h(i):
-            if i < 8:
-                cols = slice(256 * (i % 4), 256 * (i % 4 + 1))
-                codes, scale = hb_codes[i // 4][:, cols], hb_scale[i // 4][:, cols]
+            side, banks = units[i]
+            b0, n0 = banks[0]
+            if side == "b":
+                cols = slice(n0, n0 + NT * len(banks))
+                codes, scale = hb_codes[b0][:, cols], hb_scale[b0][:, cols]
             else:
-                codes, scale = ha_codes[i - 8][:], ha_scale[i - 8][:]
-            nc.vector.quantize_mx(out=codes.bitcast(FP8X4), scales=scale, in_=h[i][:])
+                cols = slice(NT * b0, NT * (b0 + len(banks)))
+                codes, scale = ha_codes[n0 // NT][:, cols], ha_scale[n0 // NT][:, cols]
+            nc.vector.quantize_mx(
+                out=codes.bitcast(FP8X4), scales=scale, in_=h[i][:].rearrange("p u n t -> p (u n t)")
+            )
+
+        def score_pass(y, m, b, cols):
+            nc.tensor.matmul_mx(
+                y[:],
+                lhsT=ha_codes[m][:, NT * b : NT * (b + 1)].bitcast(FP8X4),
+                lhsT_scale=ha_scale[m][:, NT * b : NT * (b + 1)],
+                rhs=hb_codes[b][:, cols].bitcast(FP8X4),
+                rhs_scale=hb_scale[b][:, cols],
+                start=(b == 0),
+                stop=(b == 1),
+            )
+
+        def store_scores(y, res, m, cols, on_vector):
+            if on_vector:
+                nc.vector.tensor_scalar_mul(res[:, cols], y[:], OUT_SCALE)
+            else:
+                nc.scalar.activation(res[:, cols], y[:], ACT.Copy, scale=OUT_SCALE)
+            nc.sync.dma_start(out[NT * m : NT * (m + 1), cols], res[:, cols])
 
         def scores(m):
-            res = ring.tile([P, J], F32, name="res", bufs=4)
+            res = ring.tile([P, J], F32, name="res")
             for jh in range(2):
                 cols = slice(512 * jh, 512 * (jh + 1))
                 y = ypool.tile([P, 512], F32, name="y")
                 for b in range(2):
-                    nc.tensor.matmul_mx(
-                        y[:],
-                        lhsT=ha_codes[m][:, NT * b : NT * (b + 1)].bitcast(FP8X4),
-                        lhsT_scale=ha_scale[m][:, NT * b : NT * (b + 1)],
-                        rhs=hb_codes[b][:, cols].bitcast(FP8X4),
-                        rhs_scale=hb_scale[b][:, cols],
-                        start=(b == 0),
-                        stop=(b == 1),
-                    )
-                if m == 3 and jh == 1:
-                    nc.vector.tensor_scalar_mul(res[:, cols], y[:], OUT_SCALE)
-                else:
-                    nc.scalar.activation(res[:, cols], y[:], ACT.Copy, scale=OUT_SCALE)
-                nc.sync.dma_start(out[NT * m : NT * (m + 1), cols], res[:, cols])
+                    score_pass(y, m, b, cols)
+                store_scores(y, res, m, cols, False)
 
         def order_wa_scale():
-            wa["scale"] = held("h0", [P, 2 * R], U8)
+            wa["scale"] = held("wb_bf10", [P, 2 * R], U8)
             nc.vector.tensor_copy(
                 wa["scale"][:].bitcast(I32).rearrange("p (g t q w) -> p g t q w", t=4, q=16, w=2),
                 wa_scale_raw[:].bitcast(I32).rearrange("p (g q t w) -> p g t q w", t=4, q=16, w=2),
@@ -273,37 +297,59 @@ def tile_list_biaff_silu_none_kernel(
             ga_words[a] = held(f"h{1 + 2 * a}", [P, M], U32)
             gather(ga_words[a], ta_words[a][:].bitcast(U32), list_a, 0, M)
 
-        front([0, 1])
+        first_fronts()
         back(0)
         cast_wb(0, 1)
         back(1)
         quant_h(0)
-        front([2])
+        wa["tab_scale"] = held("h0", [P, 2 * M], U8)
+        nc.gpsimd.memset(wa["tab_scale"][:].bitcast(I32), 0)
+        place_scale_rows(nc.sync, wa["tab_scale"], ga_picked)
+        front(2)
         quant_h(1)
         order_wa_scale()
         gather_a(0)
         quant_wb(0, 1)
+        sa_rows = load_factor(nc.sync, "act0", sa)
         cast_wb(1, 1)
         back(2)
-        front([3])
+        front(3)
         order_wa_codes()
         quant_h(2)
         quant_wb(1, 1)
-        front([4])
+        front(4)
         back(3)
-        front([5])
         quant_h(3)
         gather_a(1)
-        for i in range(4, 11):
-            back(i)
-            if i + 2 < 12:
-                front([i + 2])
-            if i > 4:
-                quant_h(i - 1)
-            if i > 8:
-                scores(i - 9)
-        quant_h(10)
+        front(5)
+        turn_factor(sa_rows, 0)
+        back(4)
+        front(6)
+        front(7)
+        back(5)
+        quant_h(4)
+        front(8)
+        back(6)
+        quant_h(5)
+        front(9)
+        front(10)
+        back(7)
+        quant_h(6)
+        scores(0)
+        back(8)
+        quant_h(7)
+        scores(1)
+        quant_h(8)
         scores(2)
-        back(11)
-        quant_h(11)
-        scores(3)
+        back(9)
+        back(10)
+        quant_h(9)
+        res = ring.tile([P, J], F32, name="res")
+        quarters = [slice(256 * c, 256 * (c + 1)) for c in range(4)]
+        last = [zpool.tile([P, 256], F32, name="z") for c in range(4)]
+        for c in range(4):
+            score_pass(last[c], 3, 0, quarters[c])
+        quant_h(10)
+        for c in range(4):
+            score_pass(last[c], 3, 1, quarters[c])
+            store_scores(last[c], res, 3, quarters[c], c % 2 == 1)

from contextlib import ExitStack

import concourse.mybir as mybir
from concourse.masks import make_identity

K, R, T, M, J = 1024, 1024, 2048, 512, 1024
FLOPS = 2 * K * R * M + 2 * K * R * J + 2 * R * M * J

F32 = mybir.dt.float32
BF16 = mybir.dt.bfloat16
I32 = mybir.dt.int32
U32 = mybir.dt.uint32
U16 = mybir.dt.uint16
U8 = mybir.dt.uint8
FP8X4 = mybir.dt.float8_e4m3fn_x4
FP4X4 = mybir.dt.float4_e2m1fn_x4
ACT = mybir.ActivationFunctionType
MULT = mybir.AluOpType.mult

P = 128
PASS = 512
NT = 128
OUT_SCALE = 0.03125


def tile_list_biaff_silu_none_kernel(
    tc, tab_words, tab_scales, tab2_words, tab2_scales, wa_words, wa_scales, wb, sa, sb, offs, offs2, out
):
    nc = tc.nc
    with ExitStack() as ctx:
        keep = ctx.enter_context(tc.tile_pool(name="keep", bufs=1))
        ring = ctx.enter_context(tc.tile_pool(name="ring", bufs=4))
        big = ctx.enter_context(tc.tile_pool(name="big", bufs=4))
        zpool = ctx.enter_context(tc.psum_pool(name="zpool", bufs=5))
        ypool = ctx.enter_context(tc.psum_pool(name="ypool", bufs=3))

        def held(name, shape, dtype):
            return keep.tile(shape, dtype, name=name, align_bytes=64)

        list_a = keep.tile([P, M // 16], U16, name="list_a")
        list_b = keep.tile([P, J // 16], U16, name="list_b")
        ta_scale = held("ta_scale", [P, T], U8)

        def streamed(shape, dtype):
            return big.tile(shape, dtype, name="big", align_bytes=64)

        tb_scale = streamed([P, T], U8)
        wb_raw = {}
        ta_words = {}
        tb_words = {}
        ident = held("ident", [P, P], F32)
        s_cols = held("s_cols", [P, 4, 1, 4], F32)

        def load_wb(a, b):
            wb_raw[a, b] = streamed([P, 4, PASS], F32)
            rows = wb[PASS * a : PASS * (a + 1), PASS * b : PASS * (b + 1)]
            nc.sync.dma_start(wb_raw[a, b][:], rows.rearrange("(p j) c -> p j c", j=4))

        def load_words(tiles, words, a):
            tiles[a] = streamed([P, T], I32)
            nc.sync.dma_start(tiles[a][:], words[a].rearrange("p t i -> p (t i)").bitcast(I32))

        def load_scale_rows(tile, scales):
            nc.scalar.dma_start(tile[96:P, :].bitcast(I32), scales.bitcast(I32).rearrange("a q w -> q a w"))

        def place_scale_rows(queue, plane, picked):
            for q in range(4):
                queue.dma_start(
                    plane[32 * q : 32 * q + 4, :].bitcast(I32), picked[96 + 8 * q : 96 + 8 * q + 8, :].bitcast(I32)
                )

        gb_scale = held("gb_scale", [P, 2 * J], U8)
        warm = held("warm", [P, 2], F32)

        def load_factor(queue, buf, vec):
            rows = held(buf, [P, 2 * P], F32)
            nc.gpsimd.memset(rows[:], 0.0)
            queue.dma_start(
                rows[0:4, :].rearrange("t (g i) -> t g i", i=8), vec.rearrange("(g t i) -> t g i", t=4, i=8)
            )
            return rows

        def turn_factor(rows, v):
            turned = ypool.tile([P, 2, P], F32, name="y")
            for b in range(2):
                nc.tensor.transpose(turned[:, b, :], rows[:, P * b : P * (b + 1)], ident[:])
            nc.scalar.copy(s_cols[:, 2 * v : 2 * v + 2, 0, :], turned[:, :, 0:4])

        nc.sync.dma_start(list_b[:], offs2)
        load_scale_rows(tb_scale, tab2_scales)
        load_scale_rows(ta_scale, tab_scales)
        nc.vector.memset(tb_scale[0:96, :].bitcast(I32), 0)
        nc.vector.memset(gb_scale[:].bitcast(I32), 0)
        nc.vector.memset(ta_scale[0:96, :].bitcast(I32), 0)
        nc.gpsimd.memset(warm[:], 0.0)
        nc.sync.dma_start(list_a[:], offs)
        load_wb(0, 0)
        load_words(tb_words, tab2_words, 0)
        load_wb(1, 0)
        sb_rows = load_factor(nc.scalar, "sb_rows", sb)
        nc.scalar.activation(warm[:, 0:1], warm[:, 1:2], ACT.Silu)
        make_identity(nc, ident[:])

        gb_picked = held("gb_picked", [P, J], U8)
        gb_words = [held(f"gb_words{a}", [P, J], U32) for a in range(2)]
        ga_words = {}

        def gather(dst, window, lst, lo, hi):
            nc.vector.tensor_copy(dst[:, lo:hi], window.indirect(lst[:, lo // 16 : hi // 16]))

        wb_bf = {}
        wb_codes = {(a, b): held(f"wb_codes{a}{b}", [P, PASS], U32) for a in range(2) for b in range(2)}
        wb_scale = {(a, b): held(f"wb_scale{a}{b}", [P, PASS], U8) for a in range(2) for b in range(2)}

        def cast_wb(a, b, on_vector=0):
            wb_bf[a, b] = held(f"wb_bf{a}0" if b == 0 else f"act{a}", [P, 4 * PASS], BF16)
            dst = wb_bf[a, b][:].rearrange("p (t q u i j) -> p t q u j i", t=4, u=4, i=2, j=4)
            src = wb_raw[a, b][:].rearrange("p j (q t u i) -> p t q u j i", t=4, u=4, i=2)
            for t in range(4):
                if t < 4 - on_vector:
                    nc.scalar.copy(dst[:, t], src[:, t])
                else:
                    nc.vector.tensor_copy(dst[:, t], src[:, t])

        def quant_wb(a, b):
            nc.vector.quantize_mx(out=wb_codes[a, b][:].bitcast(FP8X4), scales=wb_scale[a, b][:], in_=wb_bf[a, b][:])

        gather(gb_picked, tb_scale[:], list_b, 0, J)
        place_scale_rows(nc.sync, gb_scale, gb_picked)
        load_words(tb_words, tab2_words, 1)
        cast_wb(0, 0)
        load_wb(0, 1)
        for h in range(2):
            gather(gb_words[0], tb_words[0][:].bitcast(U32), list_b, 512 * h, 512 * (h + 1))
        load_wb(1, 1)
        quant_wb(0, 0)
        wa_scale_raw = held("wb_bf00", [P, 2 * R], U8)
        nc.gpsimd.memset(wa_scale_raw[:].bitcast(I32), 0)
        for q in range(4):
            nc.sync.dma_start(
                wa_scale_raw[32 * q : 32 * q + 4, :].bitcast(I32).rearrange("r (a w) -> r a w", a=2),
                wa_scales[:, 4 * q : 4 * q + 4, :].bitcast(I32).rearrange("a r w -> r a w"),
            )
        ga_picked = held("ga_picked", [P, M], U8)
        gather(ga_picked, ta_scale[:], list_a, 0, M)
        cast_wb(1, 0, on_vector=2)
        load_words(ta_words, tab_words, 0)
        turn_factor(sb_rows, 1)
        quant_wb(1, 0)
        for lo, hi in ((0, 256), (256, 512), (512, J)):
            gather(gb_words[1], tb_words[1][:].bitcast(U32), list_b, lo, hi)
        wa_raw = streamed([P, 2 * R // 2], I32)
        nc.sync.dma_start(
            wa_raw[:].rearrange("p (a w) -> p a w", a=2), wa_words.bitcast(I32).rearrange("a p w -> p a w")
        )
        load_words(ta_words, tab_words, 1)

        wa = {}

        def z_passes(z, side, b, n0, a):
            for t in range(4):
                if side == "b":
                    codes = wb_codes[a, b][:, P * t : P * (t + 1)].bitcast(FP8X4)
                    scale = wb_scale[a, b][:, P * t : P * (t + 1)]
                    moving = gb_words[a][:, n0 : n0 + NT]
                    moving_scale = gb_scale[:, J * a + n0 : J * a + n0 + NT]
                else:
                    c0 = R * a + PASS * b + P * t
                    codes = wa["codes"][:].bitcast(U8)[:, 2 * c0 : 2 * (c0 + P)].bitcast(FP4X4)
                    scale = wa["scale"][:, c0 : c0 + P]
                    moving = ga_words[a][:, n0 : n0 + NT]
                    moving_scale = wa["tab_scale"][:, M * a + n0 : M * a + n0 + NT]
                nc.tensor.matmul_mx(
                    z[:, t, :],
                    lhsT=codes,
                    lhsT_scale=scale,
                    rhs=moving.bitcast(FP8X4),
                    rhs_scale=moving_scale,
                    start=(a == 0 and t == 0),
                    stop=(a == 1 and t == 3),
                )

        hb_codes = [held(f"hb_codes{b}", [P, J], U32) for b in range(2)]
        hb_scale = [held(f"hb_scale{b}", [P, J], U8) for b in range(2)]
        ha_codes = [held(f"ha_codes{m}", [P, 2 * NT], U32) for m in range(4)]
        ha_scale = [held(f"ha_scale{m}", [P, 2 * NT], U8) for m in range(4)]

        units = [("b", [(0, NT * (2 * i + u)) for u in range(2)]) for i in range(4)]
        units = units + [("b", [(1, NT * (4 * i + u)) for u in range(4)]) for i in range(2)]
        units = units + [("a", [(b, NT * m) for b in range(2)]) for m in range(3)]
        units = units + [("a", [(b, NT * 3)]) for b in range(2)]
        act = {}
        h = {}

        def silu(z, i, u):
            nc.scalar.activation(act[i][:, u, :, :], z[:].rearrange("p t n -> p n t"), ACT.Silu)

        def act_tile(i):
            shape = [P, len(units[i][1]), NT, 4]
            if i < 4:
                return held(f"act{i}", shape, F32)
            return ring.tile(shape, F32, name="act", align_bytes=64)

        def front(i):
            side, banks = units[i]
            act[i] = act_tile(i)
            for u, (b, n0) in enumerate(banks):
                z = zpool.tile([P, 4, NT], F32, name="z")
                for a in range(2):
                    z_passes(z, side, b, n0, a)
                silu(z, i, u)

        def first_fronts():
            z = {}
            for i in range(2):
                act[i] = act_tile(i)
                for u, (b, n0) in enumerate(units[i][1]):
                    z[i, u] = zpool.tile([P, 4, NT], F32, name="z")
                    z_passes(z[i, u], "b", b, n0, 0)
            for i, u in z:
                b, n0 = units[i][1][u]
                z_passes(z[i, u], "b", b, n0, 1)
                silu(z[i, u], i, u)

        def back(i):
            side, banks = units[i]
            shape = [P, len(banks), NT, 4]
            if i < 4:
                h[i] = held(f"h{i}", shape, BF16)
            else:
                h[i] = ring.tile(shape, BF16, name="h", align_bytes=64)
            b0 = banks[0][0]
            if side == "b":
                factor = s_cols[:, 2 + b0, :, :].to_broadcast([P, len(banks) * NT, 4])
                nc.vector.tensor_tensor(
                    h[i][:].rearrange("p u n t -> p (u n) t"), act[i][:].rearrange("p u n t -> p (u n) t"), factor, MULT
                )
            else:
                factor = s_cols[:, b0 : b0 + len(banks), :, :].to_broadcast(shape)
                nc.vector.tensor_tensor(h[i][:], act[i][:], factor, MULT)

        def quant_h(i):
            side, banks = units[i]
            b0, n0 = banks[0]
            if side == "b":
                cols = slice(n0, n0 + NT * len(banks))
                codes, scale = hb_codes[b0][:, cols], hb_scale[b0][:, cols]
            else:
                cols = slice(NT * b0, NT * (b0 + len(banks)))
                codes, scale = ha_codes[n0 // NT][:, cols], ha_scale[n0 // NT][:, cols]
            nc.vector.quantize_mx(
                out=codes.bitcast(FP8X4), scales=scale, in_=h[i][:].rearrange("p u n t -> p (u n t)")
            )

        def score_pass(y, m, b, cols):
            nc.tensor.matmul_mx(
                y[:],
                lhsT=ha_codes[m][:, NT * b : NT * (b + 1)].bitcast(FP8X4),
                lhsT_scale=ha_scale[m][:, NT * b : NT * (b + 1)],
                rhs=hb_codes[b][:, cols].bitcast(FP8X4),
                rhs_scale=hb_scale[b][:, cols],
                start=(b == 0),
                stop=(b == 1),
            )

        def store_scores(y, res, m, cols, on_vector):
            if on_vector:
                nc.vector.tensor_scalar_mul(res[:, cols], y[:], OUT_SCALE)
            else:
                nc.scalar.activation(res[:, cols], y[:], ACT.Copy, scale=OUT_SCALE)
            nc.sync.dma_start(out[NT * m : NT * (m + 1), cols], res[:, cols])

        def scores(m):
            res = ring.tile([P, J], F32, name="res")
            for jh in range(2):
                cols = slice(512 * jh, 512 * (jh + 1))
                y = ypool.tile([P, 512], F32, name="y")
                for b in range(2):
                    score_pass(y, m, b, cols)
                store_scores(y, res, m, cols, False)

        def order_wa_scale():
            wa["scale"] = held("wb_bf10", [P, 2 * R], U8)
            nc.vector.tensor_copy(
                wa["scale"][:].bitcast(I32).rearrange("p (g t q w) -> p g t q w", t=4, q=16, w=2),
                wa_scale_raw[:].bitcast(I32).rearrange("p (g q t w) -> p g t q w", t=4, q=16, w=2),
            )

        def order_wa_codes():
            wa["codes"] = held("act2", [P, 2 * R // 2], I32)
            nc.vector.tensor_copy(
                wa["codes"][:].rearrange("p (g t q w) -> p g t q w", t=4, q=16, w=4),
                wa_raw[:].rearrange("p (g q t w) -> p g t q w", t=4, q=16, w=4),
            )

        def gather_a(a):
            ga_words[a] = held(f"h{1 + 2 * a}", [P, M], U32)
            gather(ga_words[a], ta_words[a][:].bitcast(U32), list_a, 0, M)

        first_fronts()
        back(0)
        cast_wb(0, 1)
        back(1)
        quant_h(0)
        wa["tab_scale"] = held("h0", [P, 2 * M], U8)
        nc.gpsimd.memset(wa["tab_scale"][:].bitcast(I32), 0)
        place_scale_rows(nc.sync, wa["tab_scale"], ga_picked)
        front(2)
        quant_h(1)
        order_wa_scale()
        gather_a(0)
        quant_wb(0, 1)
        sa_rows = load_factor(nc.sync, "act0", sa)
        cast_wb(1, 1)
        back(2)
        front(3)
        order_wa_codes()
        quant_h(2)
        quant_wb(1, 1)
        front(4)
        back(3)
        quant_h(3)
        gather_a(1)
        front(5)
        turn_factor(sa_rows, 0)
        back(4)
        front(6)
        front(7)
        back(5)
        quant_h(4)
        front(8)
        back(6)
        quant_h(5)
        front(9)
        front(10)
        back(7)
        quant_h(6)
        scores(0)
        back(8)
        quant_h(7)
        scores(1)
        quant_h(8)
        scores(2)
        back(9)
        back(10)
        quant_h(9)
        res = ring.tile([P, J], F32, name="res")
        quarters = [slice(256 * c, 256 * (c + 1)) for c in range(4)]
        last = [zpool.tile([P, 256], F32, name="z") for c in range(4)]
        for c in range(4):
            score_pass(last[c], 3, 0, quarters[c])
        quant_h(10)
        for c in range(4):
            score_pass(last[c], 3, 1, quarters[c])
            store_scores(last[c], res, 3, quarters[c], c % 2 == 1)
